import numpy as np, ml_dtypes
CORES = [4,12,20,28,36,44,0,8,16,24,32,40]
N = 12
KB, QP = 1, 512
def setup_inputs(rng):
    return {"q": rng.standard_normal((N, 128, QP), dtype=np.float32).astype(ml_dtypes.bfloat16), "k": rng.standard_normal((N, 128, KB * 128), dtype=np.float32).astype(ml_dtypes.bfloat16), "v": rng.standard_normal((N, 128, KB * 128), dtype=np.float32).astype(ml_dtypes.bfloat16)}
def reference(q, k, v):
    Q, K, V = q.astype(np.float64), k.astype(np.float64), v.astype(np.float64)
    y = np.zeros((N, 128, QP))
    for r in range(N):
        for j in range(N):
            for b in range(KB):
                S = np.maximum(K[j][:, 128 * b:128 * b + 128].T @ Q[r], 0.0)
                y[r] += V[j][:, 128 * b:128 * b + 128].T @ S
    return {"y": y.astype(ml_dtypes.bfloat16 if q.dtype != np.float64 else np.float64)}

@@ -1,0 +1,211 @@
+from concourse.bass import DstId, RemoteDMATransfer
+from concourse.mybir import AluOpType
+
+N = 12
+QP = 512
+HQ = QP // 2
+BW = 256
+NB = 3
+LA = 2
+FORWARD_FAR = False
+
+SCRATCH = {
+    "kv": ("sbuf", [128, N * BW], "bfloat16"),
+    "qs": ("sbuf", [128, QP], "bfloat16"),
+    "zero": ("sbuf", [128, QP], "bfloat16"),
+    "r0": ("sbuf", [128, QP], "bfloat16"),
+    "r1": ("sbuf", [128, QP], "bfloat16"),
+    "r2": ("sbuf", [128, QP], "bfloat16"),
+    "ysb": ("sbuf", [128, QP], "bfloat16"),
+    "s0": ("psum", [128, QP], "float32"),
+    "s1": ("psum", [128, QP], "float32"),
+    "s2": ("psum", [128, QP], "float32"),
+    "oa": ("psum", [128, QP], "float32"),
+    "ob": ("psum", [128, QP], "float32"),
+}
+SEMAPHORES = ["ldkv", "ldq", "sent", "zs", "ss", "sr", "so", "ya", "yb", "sta", "stb"] + ["arr%d" % j for j in range(N)]
+
+_LOAD, _ISSUE, _LAT_ON, _LAT_OFF, _W8 = 2.0, 1.0, 1.5, 2.0, 0.8
+
+
+def _bits(m):
+    return bin(m).count("1")
+
+
+def _plan(T, topo):
+    ranks = list(T.cores)
+    chips = sorted({topo.chip(c) for c in ranks})
+    cores = [c for c in range(topo.CORES_PER_CHIP * (max(chips) + 1))]
+    on_chip = {ch: [c for c in cores if topo.chip(c) == ch] for ch in chips}
+    sends, need, est, busy = {}, {}, {}, {}
+
+    def ranks_of(ch, die_first):
+        rs = [r for r in ranks if topo.chip(r) == ch]
+        return [r for r in rs if topo.die(r) == die_first] + [r for r in rs if topo.die(r) != die_first]
+
+    def post(core, j, ready, on, off):
+        m_off = topo.mask(core, off[0]) if off else 0
+        m_on = topo.mask(core, on[0]) if on else 0
+        if on and off:
+            if m_on & ~m_off:
+                m_on = m_on & ~m_off
+            else:
+                on, off, m_on = [], on + off, 0
+        t = max(ready, busy.get(core, 0.0)) + _ISSUE
+        busy[core] = t
+        parts = []
+        for m, dsts in ((m_on, on), (m_off, off)):
+            if not dsts:
+                continue
+            parts.append((m, list(dsts)))
+            for i, dcore in enumerate(dsts):
+                a, b = topo.chip(core), topo.chip(dcore)
+                lat = _LAT_ON if a == b else (_LAT_OFF if topo.same_plane(a, b) or topo.mates(a, b)
+                                              else 1.3 * _LAT_OFF)
+                need[(dcore, j)] = _bits(m)
+                est[(dcore, j)] = t + (i + 1) * _W8 * 8.0 / _bits(m) + lat
+        sends.setdefault(core, []).append((j, parts))
+
+    second = []
+    for j, s in enumerate(ranks):
+        x, d = topo.chip(s), topo.die(s)
+        est[(s, j)] = _LOAD
+        ring = sorted([x] + [c for c in chips if topo.same_plane(x, c)])
+        ix = ring.index(x)
+        near = [ring[(ix + k) % len(ring)] for k in range(1, len(ring))]
+        far = sorted(c for c in chips if c != x and not topo.same_plane(x, c))
+        im = [i for i, c in enumerate(far) if topo.mates(x, c)][0]
+        far = [far[(im + k) % len(far)] for k in range(1, len(far) + 1)]
+        ports = [c for c in on_chip[x]
+                 if c not in ranks and topo.die(c) == d and topo.may_write(c, on_chip[far[-1]][0])]
+        if FORWARD_FAR:
+            targets = [ranks_of(ch, d)[0] for ch in far]
+        else:
+            width = max(len(ranks_of(ch, d)) for ch in far)
+            targets = [ranks_of(ch, d)[i] for i in range(width) for ch in far[:-1]] + ranks_of(far[-1], d)
+        share = {p: [] for p in ports}
+        for i, t in enumerate(targets):
+            share[ports[i % len(ports)]].append(t)
+        used = [p for p in ports if share[p]]
+        sibs = [r for r in ranks_of(x, d) if r != s]
+        plane = []
+        for ch in near:
+            plane += ranks_of(ch, d)
+        post(s, j, _LOAD, used + sibs, plane)
+        for p in used:
+            second.append((p, j, share[p]))
+    for p, j, dsts in second:
+        post(p, j, est[(p, j)], [], dsts)
+    if FORWARD_FAR:
+        third = []
+        for p, j, dsts in second:
+            for r in dsts:
+                sibs = [o for o in ranks if topo.chip(o) == topo.chip(r) and o != r]
+                if sibs:
+                    third.append((est[(r, j)], r, j, sibs))
+        for ready, r, j, sibs in sorted(third):
+            post(r, j, ready, sibs, [])
+    return sends, need, est
+
+
+def rank_program(g, core, T, topo):
+    sem = T.sem
+    sends, need, est = _plan(T, topo)
+    rank = T.rank_of(core)
+
+    def slot(j):
+        return T.kv[:, j * BW:(j + 1) * BW]
+
+    def dst_id(c):
+        rid, pid, _se = topo.addr(c)
+        return DstId(rid=rid, pnc=pid)
+
+    if rank is not None:
+        g.sync.dma_start(T.kv[:, rank * BW:rank * BW + 128], T.k[:, :]).then_inc(sem.ldkv, 16)
+        g.scalar.dma_start(T.kv[:, rank * BW + 128:rank * BW + 256], T.v[:, :]).then_inc(sem.ldkv, 16)
+        g.sync.dma_start(T.qs[:, 0:HQ], T.q[:, 0:HQ]).then_inc(sem.ldq, 16)
+        g.scalar.dma_start(T.qs[:, HQ:QP], T.q[:, HQ:QP]).then_inc(sem.ldq, 16)
+
+    total = 0
+    for j, parts in sends.get(core, []):
+        if rank == j:
+            g.wait_ge(sem.ldkv, 32)
+        else:
+            g.wait_ge(sem["arr%d" % j], need[(core, j)])
+        transfers = []
+        for m, dsts in parts:
+            transfers.append(RemoteDMATransfer(dst_ids=[dst_id(c) for c in dsts], dma_engine_mask=m,
+                                               remote_sem=sem["arr%d" % j], srcs=[slot(j)],
+                                               dsts=[slot(j) for _c in dsts], alu_op=0))
+            total += _bits(m)
+        g.remote_dma_fused(transfers, local_sem=sem.sent)
+    if total:
+        g.wait_ge(sem.sent, total)
+    if rank is None:
+        return
+
+    order = sorted(range(N), key=lambda j: (est[(core, j)], j))
+    units = [(j, 0, QP) for j in order[:-1]] + [(order[-1], 0, HQ), (order[-1], HQ, QP)]
+    U = len(units)
+    ps = [T.s0, T.s1, T.s2]
+    rb = [T.r0, T.r1, T.r2]
+    acc = [T.oa, T.ob]
+    halves = [[h for h in (0, 1) if c0 <= h * HQ < c1] for (_j, c0, c1) in units]
+    so_done, n = [], 0
+    for hs in halves:
+        n += len(hs)
+        so_done.append(n)
+    first = [min(i for i in range(U) if h in halves[i]) for h in (0, 1)]
+    last = [max(i for i in range(U) if h in halves[i]) for h in (0, 1)]
+    waited = {}
+
+    def wait(qname, queue, s, v):
+        if waited.get((qname, s), 0) >= v:
+            return
+        waited[(qname, s)] = v
+        queue.wait_ge(sem[s], v)
+
+    te, ve = g.tensor, g.vector
+    for step in range(U + LA):
+        if step < U:
+            i = step
+            j, c0, c1 = units[i]
+            if j == rank:
+                wait("t", te, "ldkv", 32)
+            else:
+                wait("t", te, "arr%d" % j, need[(core, j)])
+            wait("t", te, "ldq", 32)
+            if i >= NB:
+                wait("t", te, "sr", i - NB + 1)
+            te.matmul(out=ps[i % NB][:, 0:c1 - c0], lhsT=T.kv[:, j * BW:j * BW + 128], rhs=T.qs[:, c0:c1],
+                      start=True, stop=True).then_inc(sem.ss, 1)
+        if step >= LA:
+            i = step - LA
+            j, c0, c1 = units[i]
+            wait("t", te, "sr", i + 1)
+            for h in halves[i]:
+                o = h * HQ - c0
+                te.matmul(out=acc[h][:, 0:HQ], lhsT=T.kv[:, j * BW + 128:j * BW + 256],
+                          rhs=rb[i % NB][:, o:o + HQ], start=(i == first[h]), stop=(i == last[h])
+                          ).then_inc(sem.so, 1)
+
+    ve.memset(T.zero[:, :], 0.0).then_inc(sem.zs, 1)
+    wait("v", ve, "zs", 1)
+    for i, (j, c0, c1) in enumerate(units):
+        w = c1 - c0
+        wait("v", ve, "ss", i + 1)
+        if i >= NB:
+            wait("v", ve, "so", so_done[i - NB])
+        ve.tensor_tensor(out=rb[i % NB][:, 0:w], in0=ps[i % NB][:, 0:w], in1=T.zero[:, 0:w],
+                         op=AluOpType.max).then_inc(sem.sr, 1)
+    wait("v", ve, "so", so_done[last[0]])
+    ve.tensor_copy(out=T.ysb[:, 0:HQ], in_=T.oa[:, 0:HQ]).then_inc(sem.ya, 1)
+    wait("v", ve, "so", so_done[last[1]])
+    ve.tensor_copy(out=T.ysb[:, HQ:QP], in_=T.ob[:, 0:HQ]).then_inc(sem.yb, 1)
+
+    g.sync.wait_ge(sem.ya, 1)
+    g.sync.dma_start(T.y[:, 0:HQ], T.ysb[:, 0:HQ]).then_inc(sem.sta, 16)
+    g.sync.wait_ge(sem.sta, 16)
+    g.scalar.wait_ge(sem.yb, 1)
+    g.scalar.dma_start(T.y[:, HQ:QP], T.ysb[:, HQ:QP]).then_inc(sem.stb, 16)
+    g.scalar.wait_ge(sem.stb, 16)

@@ -7,7 +7,7 @@ HQ = QP // 2
 BW = 256
 NB = 3
 LA = 2
-FORWARD_FAR = False
+FORWARD_FAR = True
 
 SCRATCH = {
     "kv": ("sbuf", [128, N * BW], "bfloat16"),

@@ -7,7 +7,6 @@ HQ = QP // 2
 BW = 256
 NB = 3
 LA = 2
-FORWARD_FAR = True
 
 SCRATCH = {
     "kv": ("sbuf", [128, N * BW], "bfloat16"),
@@ -17,15 +16,17 @@ SCRATCH = {
     "r1": ("sbuf", [128, QP], "bfloat16"),
     "r2": ("sbuf", [128, QP], "bfloat16"),
     "ysb": ("sbuf", [128, QP], "bfloat16"),
+    "pl": ("sbuf", [128, QP], "bfloat16"),
     "s0": ("psum", [128, QP], "float32"),
     "s1": ("psum", [128, QP], "float32"),
     "s2": ("psum", [128, QP], "float32"),
     "oa": ("psum", [128, QP], "float32"),
     "ob": ("psum", [128, QP], "float32"),
 }
-SEMAPHORES = ["ldkv", "ldq", "sent", "zs", "ss", "sr", "so", "ya", "yb", "sta", "stb"] + ["arr%d" % j for j in range(N)]
+SEMAPHORES = (["ldkv", "ldq", "sent", "zs", "ss", "sr", "so", "ya", "yb", "sta", "stb", "qarr", "parr"]
+              + ["arr%d" % j for j in range(N)])
 
-_LOAD, _ISSUE, _LAT_ON, _LAT_OFF, _W8 = 2.0, 1.0, 1.5, 2.0, 0.8
+_LOAD, _ISSUE, _LAT_ON, _LAT_OFF, _W8 = 2.0, 0.7, 1.0, 1.3, 0.6
 
 
 def _bits(m):
@@ -37,27 +38,32 @@ def _plan(T, topo):
     chips = sorted({topo.chip(c) for c in ranks})
     cores = [c for c in range(topo.CORES_PER_CHIP * (max(chips) + 1))]
     on_chip = {ch: [c for c in cores if topo.chip(c) == ch] for ch in chips}
-    sends, need, est, busy = {}, {}, {}, {}
+    sends, need, est, busy, partner, ports_of = {}, {}, {}, {}, {}, {}
+
+    def masks(core):
+        m_all = topo.mask(core, [c for c in on_chip[topo.chip(core)] if c != core][0])
+        m_off = topo.mask(core, [c for c in cores if topo.chip(c) != topo.chip(core)][0]) & m_all
+        return m_off, m_all & ~m_off, m_all
 
     def ranks_of(ch, die_first):
         rs = [r for r in ranks if topo.chip(r) == ch]
         return [r for r in rs if topo.die(r) == die_first] + [r for r in rs if topo.die(r) != die_first]
 
-    def post(core, j, ready, on, off):
-        m_off = topo.mask(core, off[0]) if off else 0
-        m_on = topo.mask(core, on[0]) if on else 0
-        if on and off:
-            if m_on & ~m_off:
-                m_on = m_on & ~m_off
-            else:
-                on, off, m_on = [], on + off, 0
+    def far_of(x):
+        far = sorted(c for c in chips if c != x and not topo.same_plane(x, c))
+        im = [i for i, c in enumerate(far) if topo.mates(x, c)][0]
+        return [far[(im + k) % len(far)] for k in range(1, len(far) + 1)]
+
+    for s in ranks:
+        x, d = topo.chip(s), topo.die(s)
+        idle = [c for c in on_chip[x] if c not in ranks and topo.die(c) == d]
+        ports_of[s] = [c for c in idle if topo.may_write(c, on_chip[far_of(x)[-1]][0])]
+        partner[s] = [c for c in idle if c not in ports_of[s]][0]
+
+    def post(core, j, ready, parts):
         t = max(ready, busy.get(core, 0.0)) + _ISSUE
         busy[core] = t
-        parts = []
-        for m, dsts in ((m_on, on), (m_off, off)):
-            if not dsts:
-                continue
-            parts.append((m, list(dsts)))
+        for m, dsts in parts:
             for i, dcore in enumerate(dsts):
                 a, b = topo.chip(core), topo.chip(dcore)
                 lat = _LAT_ON if a == b else (_LAT_OFF if topo.same_plane(a, b) or topo.mates(a, b)
@@ -73,45 +79,38 @@ def _plan(T, topo):
         ring = sorted([x] + [c for c in chips if topo.same_plane(x, c)])
         ix = ring.index(x)
         near = [ring[(ix + k) % len(ring)] for k in range(1, len(ring))]
-        far = sorted(c for c in chips if c != x and not topo.same_plane(x, c))
-        im = [i for i, c in enumerate(far) if topo.mates(x, c)][0]
-        far = [far[(im + k) % len(far)] for k in range(1, len(far) + 1)]
-        ports = [c for c in on_chip[x]
-                 if c not in ranks and topo.die(c) == d and topo.may_write(c, on_chip[far[-1]][0])]
-        if FORWARD_FAR:
-            targets = [ranks_of(ch, d)[0] for ch in far]
-        else:
-            width = max(len(ranks_of(ch, d)) for ch in far)
-            targets = [ranks_of(ch, d)[i] for i in range(width) for ch in far[:-1]] + ranks_of(far[-1], d)
+        far = far_of(x)
+        targets = [partner[ranks_of(ch, d)[0]] for ch in far[:-1]] + [ranks_of(far[-1], d)[0]]
+        ports = ports_of[s]
         share = {p: [] for p in ports}
         for i, t in enumerate(targets):
             share[ports[i % len(ports)]].append(t)
         used = [p for p in ports if share[p]]
-        sibs = [r for r in ranks_of(x, d) if r != s]
         plane = []
         for ch in near:
             plane += ranks_of(ch, d)
-        post(s, j, _LOAD, used + sibs, plane)
+        m_off, m_on, _m_all = masks(s)
+        post(s, j, _LOAD, [(m_on, used), (m_off, plane + [r for r in ranks_of(x, d) if r != s])])
         for p in used:
             second.append((p, j, share[p]))
+    third = []
     for p, j, dsts in second:
-        post(p, j, est[(p, j)], [], dsts)
-    if FORWARD_FAR:
-        third = []
-        for p, j, dsts in second:
-            for r in dsts:
-                sibs = [o for o in ranks if topo.chip(o) == topo.chip(r) and o != r]
-                if sibs:
-                    third.append((est[(r, j)], r, j, sibs))
-        for ready, r, j, sibs in sorted(third):
-            post(r, j, ready, sibs, [])
-    return sends, need, est
+        post(p, j, est[(p, j)], [(masks(p)[0], dsts)])
+        for c in dsts:
+            others = [o for o in ranks if topo.chip(o) == topo.chip(c) and topo.die(o) != topo.die(c)]
+            if others:
+                third.append((est[(c, j)], c, j, others))
+    for ready, c, j, others in sorted(third):
+        post(c, j, ready, [(masks(c)[2], others)])
+    return sends, need, est, partner, masks
 
 
 def rank_program(g, core, T, topo):
     sem = T.sem
-    sends, need, est = _plan(T, topo)
+    sends, need, est, partner, masks = _plan(T, topo)
     rank = T.rank_of(core)
+    boss = [r for r in T.cores if partner[r] == core]
+    boss = boss[0] if boss else None
 
     def slot(j):
         return T.kv[:, j * BW:(j + 1) * BW]
@@ -139,12 +138,19 @@ def rank_program(g, core, T, topo):
                                                dsts=[slot(j) for _c in dsts], alu_op=0))
             total += _bits(m)
         g.remote_dma_fused(transfers, local_sem=sem.sent)
-    if total:
-        g.wait_ge(sem.sent, total)
-    if rank is None:
+        if rank == j:
+            m_on = masks(core)[1]
+            rid, pid, _se = topo.addr(partner[core])
+            g.wait_ge(sem.ldq, 32)
+            g.remote_dma(out_ap=T.qs[:, :], in_ap=T.qs[:, :], remote_sem=sem.qarr, local_sem=sem.sent,
+                         pid=pid, routing_id=rid, dma_engine_mask=m_on)
+            total += _bits(m_on)
+    if rank is None and boss is None:
+        if total:
+            g.wait_ge(sem.sent, total)
         return
 
-    order = sorted(range(N), key=lambda j: (est[(core, j)], j))
+    order = sorted([j for j in range(N) if (core, j) in est], key=lambda j: (est[(core, j)], j))
     units = [(j, 0, QP) for j in order[:-1]] + [(order[-1], 0, HQ), (order[-1], HQ, QP)]
     U = len(units)
     ps = [T.s0, T.s1, T.s2]
@@ -174,7 +180,10 @@ def rank_program(g, core, T, topo):
                 wait("t", te, "ldkv", 32)
             else:
                 wait("t", te, "arr%d" % j, need[(core, j)])
-            wait("t", te, "ldq", 32)
+            if rank is not None:
+                wait("t", te, "ldq", 32)
+            else:
+                wait("t", te, "qarr", _bits(masks(boss)[1]))
             if i >= NB:
                 wait("t", te, "sr", i - NB + 1)
             te.matmul(out=ps[i % NB][:, 0:c1 - c0], lhsT=T.kv[:, j * BW:j * BW + 128], rhs=T.qs[:, c0:c1],
@@ -198,11 +207,26 @@ def rank_program(g, core, T, topo):
             wait("v", ve, "so", so_done[i - NB])
         ve.tensor_tensor(out=rb[i % NB][:, 0:w], in0=ps[i % NB][:, 0:w], in1=T.zero[:, 0:w],
                          op=AluOpType.max).then_inc(sem.sr, 1)
-    wait("v", ve, "so", so_done[last[0]])
-    ve.tensor_copy(out=T.ysb[:, 0:HQ], in_=T.oa[:, 0:HQ]).then_inc(sem.ya, 1)
-    wait("v", ve, "so", so_done[last[1]])
-    ve.tensor_copy(out=T.ysb[:, HQ:QP], in_=T.ob[:, 0:HQ]).then_inc(sem.yb, 1)
+    for h, done in ((0, sem.ya), (1, sem.yb)):
+        wait("v", ve, "so", so_done[last[h]])
+        if rank is None:
+            ve.tensor_copy(out=T.ysb[:, h * HQ:(h + 1) * HQ], in_=acc[h][:, 0:HQ]).then_inc(done, 1)
+        else:
+            wait("v", ve, "parr", _bits(masks(partner[core])[2]))
+            ve.tensor_tensor(out=T.ysb[:, h * HQ:(h + 1) * HQ], in0=acc[h][:, 0:HQ],
+                             in1=T.pl[:, h * HQ:(h + 1) * HQ], op=AluOpType.add).then_inc(done, 1)
 
+    if rank is None:
+        rid, pid, _se = topo.addr(boss)
+        m_all = masks(core)[2]
+        g.wait_ge(sem.ya, 1)
+        g.wait_ge(sem.yb, 1)
+        g.remote_dma(out_ap=T.pl[:, :], in_ap=T.ysb[:, :], remote_sem=sem.parr, local_sem=sem.sent,
+                     pid=pid, routing_id=rid, dma_engine_mask=m_all)
+        g.wait_ge(sem.sent, total + _bits(m_all))
+        return
+
+    g.wait_ge(sem.sent, total)
     g.sync.wait_ge(sem.ya, 1)
     g.sync.dma_start(T.y[:, 0:HQ], T.ysb[:, 0:HQ]).then_inc(sem.sta, 16)
     g.sync.wait_ge(sem.sta, 16)

@@ -73,6 +73,7 @@ def _plan(T, topo):
         sends.setdefault(core, []).append((j, parts))
 
     second = []
+    landed = []
     for j, s in enumerate(ranks):
         x, d = topo.chip(s), topo.die(s)
         est[(s, j)] = _LOAD
@@ -86,20 +87,20 @@ def _plan(T, topo):
         for i, t in enumerate(targets):
             share[ports[i % len(ports)]].append(t)
         used = [p for p in ports if share[p]]
-        plane = []
-        for ch in near:
-            plane += ranks_of(ch, d)
+        plane = [ranks_of(ch, d)[0] for ch in near]
         m_off, m_on, _m_all = masks(s)
         post(s, j, _LOAD, [(m_on, used), (m_off, plane + [r for r in ranks_of(x, d) if r != s])])
+        landed += [(c, j) for c in plane]
         for p in used:
             second.append((p, j, share[p]))
-    third = []
     for p, j, dsts in second:
         post(p, j, est[(p, j)], [(masks(p)[0], dsts)])
-        for c in dsts:
-            others = [o for o in ranks if topo.chip(o) == topo.chip(c) and topo.die(o) != topo.die(c)]
-            if others:
-                third.append((est[(c, j)], c, j, others))
+        landed += [(c, j) for c in dsts]
+    third = []
+    for c, j in landed:
+        others = [o for o in ranks if topo.chip(o) == topo.chip(c) and topo.die(o) != topo.die(c)]
+        if others:
+            third.append((est[(c, j)], c, j, others))
     for ready, c, j, others in sorted(third):
         post(c, j, ready, [(masks(c)[2], others)])
     return sends, need, est, partner, masks

from concourse.bass import DstId, RemoteDMATransfer
from concourse.mybir import AluOpType

N = 12
QP = 512
HQ = QP // 2
BW = 256
NB = 3
LA = 2

SCRATCH = {
    "kv": ("sbuf", [128, N * BW], "bfloat16"),
    "qs": ("sbuf", [128, QP], "bfloat16"),
    "zero": ("sbuf", [128, QP], "bfloat16"),
    "r0": ("sbuf", [128, QP], "bfloat16"),
    "r1": ("sbuf", [128, QP], "bfloat16"),
    "r2": ("sbuf", [128, QP], "bfloat16"),
    "ysb": ("sbuf", [128, QP], "bfloat16"),
    "pl": ("sbuf", [128, QP], "bfloat16"),
    "s0": ("psum", [128, QP], "float32"),
    "s1": ("psum", [128, QP], "float32"),
    "s2": ("psum", [128, QP], "float32"),
    "oa": ("psum", [128, QP], "float32"),
    "ob": ("psum", [128, QP], "float32"),
}
SEMAPHORES = (["ldkv", "ldq", "sent", "zs", "ss", "sr", "so", "ya", "yb", "sta", "stb", "qarr", "parr"]
              + ["arr%d" % j for j in range(N)])

_LOAD, _ISSUE, _LAT_ON, _LAT_OFF, _W8 = 2.0, 0.7, 1.0, 1.3, 0.6


def _bits(m):
    return bin(m).count("1")


def _plan(T, topo):
    ranks = list(T.cores)
    chips = sorted({topo.chip(c) for c in ranks})
    cores = [c for c in range(topo.CORES_PER_CHIP * (max(chips) + 1))]
    on_chip = {ch: [c for c in cores if topo.chip(c) == ch] for ch in chips}
    sends, need, est, busy, partner, ports_of = {}, {}, {}, {}, {}, {}

    def masks(core):
        m_all = topo.mask(core, [c for c in on_chip[topo.chip(core)] if c != core][0])
        m_off = topo.mask(core, [c for c in cores if topo.chip(c) != topo.chip(core)][0]) & m_all
        return m_off, m_all & ~m_off, m_all

    def ranks_of(ch, die_first):
        rs = [r for r in ranks if topo.chip(r) == ch]
        return [r for r in rs if topo.die(r) == die_first] + [r for r in rs if topo.die(r) != die_first]

    def far_of(x):
        far = sorted(c for c in chips if c != x and not topo.same_plane(x, c))
        im = [i for i, c in enumerate(far) if topo.mates(x, c)][0]
        return [far[(im + k) % len(far)] for k in range(1, len(far) + 1)]

    for s in ranks:
        x, d = topo.chip(s), topo.die(s)
        idle = [c for c in on_chip[x] if c not in ranks and topo.die(c) == d]
        ports_of[s] = [c for c in idle if topo.may_write(c, on_chip[far_of(x)[-1]][0])]
        partner[s] = [c for c in idle if c not in ports_of[s]][0]

    def post(core, j, ready, parts):
        t = max(ready, busy.get(core, 0.0)) + _ISSUE
        busy[core] = t
        for m, dsts in parts:
            for i, dcore in enumerate(dsts):
                a, b = topo.chip(core), topo.chip(dcore)
                lat = _LAT_ON if a == b else (_LAT_OFF if topo.same_plane(a, b) or topo.mates(a, b)
                                              else 1.3 * _LAT_OFF)
                need[(dcore, j)] = _bits(m)
                est[(dcore, j)] = t + (i + 1) * _W8 * 8.0 / _bits(m) + lat
        sends.setdefault(core, []).append((j, parts))

    second = []
    landed = []
    for j, s in enumerate(ranks):
        x, d = topo.chip(s), topo.die(s)
        est[(s, j)] = _LOAD
        ring = sorted([x] + [c for c in chips if topo.same_plane(x, c)])
        ix = ring.index(x)
        near = [ring[(ix + k) % len(ring)] for k in range(1, len(ring))]
        far = far_of(x)
        targets = [partner[ranks_of(ch, d)[0]] for ch in far[:-1]] + [ranks_of(far[-1], d)[0]]
        ports = ports_of[s]
        share = {p: [] for p in ports}
        for i, t in enumerate(targets):
            share[ports[i % len(ports)]].append(t)
        used = [p for p in ports if share[p]]
        plane = [ranks_of(ch, d)[0] for ch in near]
        m_off, m_on, _m_all = masks(s)
        post(s, j, _LOAD, [(m_on, used), (m_off, plane + [r for r in ranks_of(x, d) if r != s])])
        landed += [(c, j) for c in plane]
        for p in used:
            second.append((p, j, share[p]))
    for p, j, dsts in second:
        post(p, j, est[(p, j)], [(masks(p)[0], dsts)])
        landed += [(c, j) for c in dsts]
    third = []
    for c, j in landed:
        others = [o for o in ranks if topo.chip(o) == topo.chip(c) and topo.die(o) != topo.die(c)]
        if others:
            third.append((est[(c, j)], c, j, others))
    for ready, c, j, others in sorted(third):
        post(c, j, ready, [(masks(c)[2], others)])
    return sends, need, est, partner, masks


def rank_program(g, core, T, topo):
    sem = T.sem
    sends, need, est, partner, masks = _plan(T, topo)
    rank = T.rank_of(core)
    boss = [r for r in T.cores if partner[r] == core]
    boss = boss[0] if boss else None

    def slot(j):
        return T.kv[:, j * BW:(j + 1) * BW]

    def dst_id(c):
        rid, pid, _se = topo.addr(c)
        return DstId(rid=rid, pnc=pid)

    if rank is not None:
        g.sync.dma_start(T.kv[:, rank * BW:rank * BW + 128], T.k[:, :]).then_inc(sem.ldkv, 16)
        g.scalar.dma_start(T.kv[:, rank * BW + 128:rank * BW + 256], T.v[:, :]).then_inc(sem.ldkv, 16)
        g.sync.dma_start(T.qs[:, 0:HQ], T.q[:, 0:HQ]).then_inc(sem.ldq, 16)
        g.scalar.dma_start(T.qs[:, HQ:QP], T.q[:, HQ:QP]).then_inc(sem.ldq, 16)

    total = 0
    for j, parts in sends.get(core, []):
        if rank == j:
            g.wait_ge(sem.ldkv, 32)
        else:
            g.wait_ge(sem["arr%d" % j], need[(core, j)])
        transfers = []
        for m, dsts in parts:
            transfers.append(RemoteDMATransfer(dst_ids=[dst_id(c) for c in dsts], dma_engine_mask=m,
                                               remote_sem=sem["arr%d" % j], srcs=[slot(j)],
                                               dsts=[slot(j) for _c in dsts], alu_op=0))
            total += _bits(m)
        g.remote_dma_fused(transfers, local_sem=sem.sent)
        if rank == j:
            m_on = masks(core)[1]
            rid, pid, _se = topo.addr(partner[core])
            g.wait_ge(sem.ldq, 32)
            g.remote_dma(out_ap=T.qs[:, :], in_ap=T.qs[:, :], remote_sem=sem.qarr, local_sem=sem.sent,
                         pid=pid, routing_id=rid, dma_engine_mask=m_on)
            total += _bits(m_on)
    if rank is None and boss is None:
        if total:
            g.wait_ge(sem.sent, total)
        return

    order = sorted([j for j in range(N) if (core, j) in est], key=lambda j: (est[(core, j)], j))
    units = [(j, 0, QP) for j in order[:-1]] + [(order[-1], 0, HQ), (order[-1], HQ, QP)]
    U = len(units)
    ps = [T.s0, T.s1, T.s2]
    rb = [T.r0, T.r1, T.r2]
    acc = [T.oa, T.ob]
    halves = [[h for h in (0, 1) if c0 <= h * HQ < c1] for (_j, c0, c1) in units]
    so_done, n = [], 0
    for hs in halves:
        n += len(hs)
        so_done.append(n)
    first = [min(i for i in range(U) if h in halves[i]) for h in (0, 1)]
    last = [max(i for i in range(U) if h in halves[i]) for h in (0, 1)]
    waited = {}

    def wait(qname, queue, s, v):
        if waited.get((qname, s), 0) >= v:
            return
        waited[(qname, s)] = v
        queue.wait_ge(sem[s], v)

    te, ve = g.tensor, g.vector
    for step in range(U + LA):
        if step < U:
            i = step
            j, c0, c1 = units[i]
            if j == rank:
                wait("t", te, "ldkv", 32)
            else:
                wait("t", te, "arr%d" % j, need[(core, j)])
            if rank is not None:
                wait("t", te, "ldq", 32)
            else:
                wait("t", te, "qarr", _bits(masks(boss)[1]))
            if i >= NB:
                wait("t", te, "sr", i - NB + 1)
            te.matmul(out=ps[i % NB][:, 0:c1 - c0], lhsT=T.kv[:, j * BW:j * BW + 128], rhs=T.qs[:, c0:c1],
                      start=True, stop=True).then_inc(sem.ss, 1)
        if step >= LA:
            i = step - LA
            j, c0, c1 = units[i]
            wait("t", te, "sr", i + 1)
            for h in halves[i]:
                o = h * HQ - c0
                te.matmul(out=acc[h][:, 0:HQ], lhsT=T.kv[:, j * BW + 128:j * BW + 256],
                          rhs=rb[i % NB][:, o:o + HQ], start=(i == first[h]), stop=(i == last[h])
                          ).then_inc(sem.so, 1)

    ve.memset(T.zero[:, :], 0.0).then_inc(sem.zs, 1)
    wait("v", ve, "zs", 1)
    for i, (j, c0, c1) in enumerate(units):
        w = c1 - c0
        wait("v", ve, "ss", i + 1)
        if i >= NB:
            wait("v", ve, "so", so_done[i - NB])
        ve.tensor_tensor(out=rb[i % NB][:, 0:w], in0=ps[i % NB][:, 0:w], in1=T.zero[:, 0:w],
                         op=AluOpType.max).then_inc(sem.sr, 1)
    for h, done in ((0, sem.ya), (1, sem.yb)):
        wait("v", ve, "so", so_done[last[h]])
        if rank is None:
            ve.tensor_copy(out=T.ysb[:, h * HQ:(h + 1) * HQ], in_=acc[h][:, 0:HQ]).then_inc(done, 1)
        else:
            wait("v", ve, "parr", _bits(masks(partner[core])[2]))
            ve.tensor_tensor(out=T.ysb[:, h * HQ:(h + 1) * HQ], in0=acc[h][:, 0:HQ],
                             in1=T.pl[:, h * HQ:(h + 1) * HQ], op=AluOpType.add).then_inc(done, 1)

    if rank is None:
        rid, pid, _se = topo.addr(boss)
        m_all = masks(core)[2]
        g.wait_ge(sem.ya, 1)
        g.wait_ge(sem.yb, 1)
        g.remote_dma(out_ap=T.pl[:, :], in_ap=T.ysb[:, :], remote_sem=sem.parr, local_sem=sem.sent,
                     pid=pid, routing_id=rid, dma_engine_mask=m_all)
        g.wait_ge(sem.sent, total + _bits(m_all))
        return

    g.wait_ge(sem.sent, total)
    g.sync.wait_ge(sem.ya, 1)
    g.sync.dma_start(T.y[:, 0:HQ], T.ysb[:, 0:HQ]).then_inc(sem.sta, 16)
    g.sync.wait_ge(sem.sta, 16)
    g.scalar.wait_ge(sem.yb, 1)
    g.scalar.dma_start(T.y[:, HQ:QP], T.ysb[:, HQ:QP]).then_inc(sem.stb, 16)
    g.scalar.wait_ge(sem.stb, 16)
